import numpy as np, ml_dtypes
CORES = [29,45,93,109,157,173,221,237,285,301,349,365,413,429,477,493]
N = 16
F = 32
BETA, LR = 0.75, 0.5
def setup_inputs(rng):
    return {"gr": rng.standard_normal((N, 128, N * F), dtype=np.float32).astype(ml_dtypes.bfloat16), "m": rng.standard_normal((N, 128, F), dtype=np.float32).astype(ml_dtypes.bfloat16), "w": rng.standard_normal((N, 128, F), dtype=np.float32).astype(ml_dtypes.bfloat16)}
def setup_inputs_big(rng):
    d = setup_inputs(rng)
    for k in ("gr", "m", "w"): d[k] = (d[k].astype(np.float32) * 1048576.0).astype(d[k].dtype)
    return d
def setup_inputs_small(rng):
    d = setup_inputs(rng)
    for k in ("gr", "m", "w"): d[k] = (d[k].astype(np.float32) * (1 / 1048576.0)).astype(d[k].dtype)
    return d
def setup_inputs_apart(rng):
    d = setup_inputs(rng)
    f = (10.0 ** rng.permutation(np.linspace(-1.5, 1.5, N))).astype(np.float32).reshape(N, 1, 1)
    for k in ("gr", "m", "w"): d[k] = (d[k].astype(np.float32) * f).astype(d[k].dtype)
    return d
def reference(gr, m, w):
    GR, M, W = gr.astype(np.float64), m.astype(np.float64), w.astype(np.float64)
    s = GR.sum(axis=0)
    m2 = np.stack([BETA * M[r] + s[:, F * r:F * r + F] for r in range(N)])
    w2 = np.concatenate([W[r] - LR * m2[r] for r in range(N)], axis=1)
    return {"y": np.broadcast_to(w2.astype(ml_dtypes.bfloat16), (N, 128, N * F)), "mo": m2.astype(ml_dtypes.bfloat16)}

@@ -1,0 +1,148 @@
+from concourse.bass import DstId, RemoteDMATransfer
+from concourse.mybir import AluOpType
+
+P = 128
+N = 16
+F = 32
+PIECES = 8
+PW = P * N * F // PIECES // P
+
+SCRATCH = {
+    "gin": ("sbuf", [P, N * F], "bfloat16"),
+    "gsc": ("sbuf", [P, N * F], "bfloat16"),
+    "msb": ("sbuf", [P, F], "bfloat16"),
+    "wsb": ("sbuf", [P, F], "bfloat16"),
+    "kh": ("psum", [P, N * F], "float32"),
+    "km": ("sbuf", [P, F], "float32"),
+    "t1": ("sbuf", [P, F], "float32"),
+    "bb": ("sbuf", [P, F], "float32"),
+    "t2": ("sbuf", [P, F], "float32"),
+    "yb": ("sbuf", [P, F], "bfloat16"),
+    "dd": ("sbuf", [P, F], "float32"),
+    "mob": ("sbuf", [P, F], "bfloat16"),
+    "dsl": ("dram", [PIECES * P, PW], "bfloat16"),
+    "l1": ("dram", [(PIECES - 1) * P, PW], "bfloat16"),
+    "cab": ("dram", [P, PW], "bfloat16"),
+    "yall": ("dram", [PIECES * P, PW], "bfloat16"),
+}
+SEMAPHORES = ["ldg", "ldmw", "vec", "std", "a1", "a2", "a3", "snt", "ldb", "sty", "stm"]
+
+
+def _bits(mask):
+    return [1 << e for e in range(16) if (mask >> e) & 1]
+
+
+def _count(mask):
+    return len(_bits(mask))
+
+
+def rank_program(g, core, T, topo):
+    rank = T.rank_of(core)
+    if rank is None:
+        return
+    cores = list(T.cores)
+    S = T.sem
+
+    def rack_of(c):
+        return topo.rack(topo.host(c))
+
+    def cable_peer(c):
+        return [d for d in cores
+                if rack_of(d) != rack_of(c) and topo.chip(d) == topo.chip(c) and topo.may_write(c, d)][0]
+
+    q = {}
+    for c in cores:
+        if rack_of(c) == rack_of(cores[0]):
+            q[c] = len(q)
+    for c in cores:
+        if c not in q:
+            q[c] = q[cable_peer(c)]
+    peers = [c for c in cores if c != core and topo.same_plane(core, c)]
+    far = cable_peer(core)
+    me = q[core]
+
+    def piece(buf, k):
+        return buf[k * P:(k + 1) * P, :]
+
+    def slot(sender, receiver):
+        return q[sender] - (1 if q[sender] > q[receiver] else 0)
+
+    def dst_id(d):
+        rid, pid = topo.addr(d, core)
+        return DstId(rid=rid, pnc=pid)
+
+    c0 = rank * F
+    v = g.vector
+    nv = [0]
+
+    def done(ins):
+        ins.then_inc(S.vec, 1)
+        nv[0] += 1
+
+    g.sync.dma_start(T.gin[:], T.gr[:]).then_inc(S.ldg, 16)
+    g.scalar.dma_start(T.msb[:], T.m[:]).then_inc(S.ldmw, 16)
+    g.scalar.dma_start(T.wsb[:], T.w[:]).then_inc(S.ldmw, 16)
+
+    done(v.memset(T.km[:], -0.375))
+    done(v.memset(T.kh[:], -0.5))
+    v.wait_ge(S.vec, nv[0])
+    v.wait_ge(S.ldmw, 32)
+    done(v.tensor_tensor(T.t1[:], T.msb[:], T.km[:], AluOpType.mult))
+    v.wait_ge(S.vec, nv[0])
+    done(v.tensor_tensor(T.bb[:], T.t1[:], T.wsb[:], AluOpType.add))
+    v.wait_ge(S.ldg, 16)
+    done(v.tensor_tensor(T.t2[:], T.gin[:, c0:c0 + F], T.kh[:, c0:c0 + F], AluOpType.mult))
+    if c0 > 0:
+        done(v.tensor_tensor(T.gsc[:, 0:c0], T.gin[:, 0:c0], T.kh[:, 0:c0], AluOpType.mult))
+    if c0 + F < N * F:
+        done(v.tensor_tensor(T.gsc[:, c0 + F:], T.gin[:, c0 + F:], T.kh[:, c0 + F:], AluOpType.mult))
+    v.wait_ge(S.vec, nv[0])
+    done(v.tensor_tensor(T.gsc[:, c0:c0 + F], T.t2[:], T.bb[:], AluOpType.add))
+
+    g.sync.wait_ge(S.vec, nv[0])
+    g.sync.dma_start(T.dsl[:], T.gsc[:]).then_inc(S.std, 16)
+
+    sent = 0
+    g.wait_ge(S.std, 16)
+    tr = []
+    for k, d in enumerate(peers):
+        eng = _bits(topo.mask(core, d))[k]
+        tr.append(RemoteDMATransfer(dst_ids=[dst_id(d)], dma_engine_mask=eng, remote_sem=S.a1,
+                                    src=piece(T.dsl, q[d]), dst=piece(T.l1, slot(core, d))))
+        sent += 1
+    g.remote_dma_fused(tr, local_sem=S.snt)
+
+    mine = [piece(T.l1, k) for k in range(PIECES - 1)] + [piece(T.dsl, me)]
+    g.wait_ge(S.a1, len(peers))
+    mfar = topo.mask(core, far)
+    g.remote_dma_fused([RemoteDMATransfer(dst_ids=[dst_id(far)], dma_engine_mask=mfar, remote_sem=S.a2,
+                                          srcs=mine, dsts=[T.cab[:]], alu_op=1)], local_sem=S.snt)
+    sent += _count(mfar)
+
+    g.wait_ge(S.a2, _count(topo.mask(far, core)))
+    outs = peers + [far]
+    mall = mfar
+    for d in outs:
+        mall &= topo.mask(core, d)
+    g.remote_dma_fused([RemoteDMATransfer(dst_ids=[dst_id(d) for d in outs], dma_engine_mask=mall, remote_sem=S.a3,
+                                          srcs=mine + [T.cab[:]], dsts=[piece(T.yall, me) for d in outs], alu_op=1)],
+                       local_sem=S.snt)
+    sent += _count(mall)
+
+    got = len(outs) * _count(mall)
+    g.sync.wait_ge(S.a3, got)
+    g.sync.dma_start(T.y[:], T.yall[:]).then_inc(S.sty, 16)
+    per_row = N * F // PW
+    g.scalar.wait_ge(S.a3, got)
+    a0, b0 = c0 // PW, c0 % PW
+    g.scalar.dma_start(T.yb[:], T.yall[a0::per_row, b0:b0 + F]).then_inc(S.ldb, 16)
+    v.wait_ge(S.ldb, 16)
+    done(v.tensor_tensor(T.dd[:], T.wsb[:], T.yb[:], AluOpType.subtract))
+    v.wait_ge(S.vec, nv[0])
+    done(v.tensor_tensor(T.mob[:], T.dd[:], T.dd[:], AluOpType.add))
+    g.scalar.wait_ge(S.vec, nv[0])
+    g.scalar.dma_start(T.mo[:], T.mob[:]).then_inc(S.stm, 16)
+
+    g.wait_ge(S.snt, sent)
+    g.wait_ge(S.sty, 16)
+    g.wait_ge(S.stm, 16)

@@ -4,36 +4,34 @@ from concourse.mybir import AluOpType
 P = 128
 N = 16
 F = 32
+H = 2
+HW = N * F // H
 PIECES = 8
-PW = P * N * F // PIECES // P
+PW = HW // PIECES
+HR = PIECES * P
 
 SCRATCH = {
-    "gin": ("sbuf", [P, N * F], "bfloat16"),
-    "gsc": ("sbuf", [P, N * F], "bfloat16"),
-    "msb": ("sbuf", [P, F], "bfloat16"),
-    "wsb": ("sbuf", [P, F], "bfloat16"),
+    "mw": ("sbuf", [P, 2 * F], "bfloat16"),
+    "gb": ("sbuf", [P, F], "bfloat16"),
+    "kk": ("psum", [P, 2 * F], "float32"),
     "kh": ("psum", [P, N * F], "float32"),
-    "km": ("sbuf", [P, F], "float32"),
-    "t1": ("sbuf", [P, F], "float32"),
-    "bb": ("sbuf", [P, F], "float32"),
-    "t2": ("sbuf", [P, F], "float32"),
-    "yb": ("sbuf", [P, F], "bfloat16"),
-    "dd": ("sbuf", [P, F], "float32"),
+    "xx": ("sbuf", [P, 2 * F], "float32"),
+    "cc": ("sbuf", [P, F], "float32"),
+    "eb": ("sbuf", [P, F], "bfloat16"),
+    "tt": ("sbuf", [P, N * F], "bfloat16"),
+    "ysb": ("sbuf", [P, N * F], "bfloat16"),
     "mob": ("sbuf", [P, F], "bfloat16"),
-    "dsl": ("dram", [PIECES * P, PW], "bfloat16"),
-    "l1": ("dram", [(PIECES - 1) * P, PW], "bfloat16"),
-    "cab": ("dram", [P, PW], "bfloat16"),
-    "yall": ("dram", [PIECES * P, PW], "bfloat16"),
+    "dsl": ("dram", [H * HR, PW], "bfloat16"),
+    "l1": ("dram", [H * (PIECES - 1) * P, PW], "bfloat16"),
+    "cab": ("dram", [H * P, PW], "bfloat16"),
+    "tall": ("dram", [H * HR, PW], "bfloat16"),
 }
-SEMAPHORES = ["ldg", "ldmw", "vec", "std", "a1", "a2", "a3", "snt", "ldb", "sty", "stm"]
+SEMAPHORES = ["lmw", "lgb", "cpe", "cpl", "vec", "ve", "stb", "a1", "a2", "a3", "snt",
+              "ld0", "ld1", "p0", "p1", "pm", "sty", "stm"]
 
 
 def _bits(mask):
     return [1 << e for e in range(16) if (mask >> e) & 1]
-
-
-def _count(mask):
-    return len(_bits(mask))
 
 
 def rank_program(g, core, T, topo):
@@ -50,6 +48,9 @@ def rank_program(g, core, T, topo):
         return [d for d in cores
                 if rack_of(d) != rack_of(c) and topo.chip(d) == topo.chip(c) and topo.may_write(c, d)][0]
 
+    def rack_peers(c):
+        return [d for d in cores if d != c and topo.same_plane(c, d)]
+
     q = {}
     for c in cores:
         if rack_of(c) == rack_of(cores[0]):
@@ -57,12 +58,12 @@ def rank_program(g, core, T, topo):
     for c in cores:
         if c not in q:
             q[c] = q[cable_peer(c)]
-    peers = [c for c in cores if c != core and topo.same_plane(core, c)]
+    peers = rack_peers(core)
     far = cable_peer(core)
     me = q[core]
 
-    def piece(buf, k):
-        return buf[k * P:(k + 1) * P, :]
+    def piece(buf, h, k, n=PIECES):
+        return buf[(h * n + k) * P:(h * n + k + 1) * P, :]
 
     def slot(sender, receiver):
         return q[sender] - (1 if q[sender] > q[receiver] else 0)
@@ -71,78 +72,90 @@ def rank_program(g, core, T, topo):
         rid, pid = topo.addr(d, core)
         return DstId(rid=rid, pnc=pid)
 
+    def engines(s, d):
+        ps = rack_peers(s)
+        b = _bits(topo.mask(s, d))
+        k = ps.index(d)
+        return b[k:] if k == len(ps) - 1 else b[k:k + 1]
+
     c0 = rank * F
+    late = c0 // HW
+    early = 1 - late
     v = g.vector
-    nv = [0]
 
-    def done(ins):
-        ins.then_inc(S.vec, 1)
-        nv[0] += 1
+    g.sync.dma_start(T.mw[:, 0:F], T.m[:]).then_inc(S.lmw, 16)
+    g.scalar.dma_start(T.mw[:, F:2 * F], T.w[:]).then_inc(S.lmw, 16)
+    g.scalar.dma_start(T.gb[:], T.gr[:, c0:c0 + F]).then_inc(S.lgb, 16)
+    g.sync.dma_start(T.dsl[early * HR:(early + 1) * HR, :], T.gr[:, early * HW:(early + 1) * HW]).then_inc(S.cpe, 16)
+    g.scalar.dma_start(T.dsl[late * HR:(late + 1) * HR, :], T.gr[:, late * HW:(late + 1) * HW]).then_inc(S.cpl, 16)
 
-    g.sync.dma_start(T.gin[:], T.gr[:]).then_inc(S.ldg, 16)
-    g.scalar.dma_start(T.msb[:], T.m[:]).then_inc(S.ldmw, 16)
-    g.scalar.dma_start(T.wsb[:], T.w[:]).then_inc(S.ldmw, 16)
+    v.memset(T.kk[:, 0:F], 0.75).then_inc(S.vec, 1)
+    v.memset(T.kk[:, F:2 * F], -2.0).then_inc(S.vec, 1)
+    v.memset(T.kh[:], -0.5).then_inc(S.vec, 1)
+    v.wait_ge(S.vec, 3)
+    v.wait_ge(S.lmw, 32)
+    v.tensor_tensor(T.xx[:], T.mw[:], T.kk[:], AluOpType.mult).then_inc(S.vec, 1)
+    v.wait_ge(S.vec, 4)
+    v.tensor_tensor(T.cc[:], T.xx[:, 0:F], T.xx[:, F:2 * F], AluOpType.add).then_inc(S.vec, 1)
+    v.wait_ge(S.vec, 5)
+    v.wait_ge(S.lgb, 16)
+    v.tensor_tensor(T.eb[:], T.gb[:], T.cc[:], AluOpType.add).then_inc(S.ve, 1)
 
-    done(v.memset(T.km[:], -0.375))
-    done(v.memset(T.kh[:], -0.5))
-    v.wait_ge(S.vec, nv[0])
-    v.wait_ge(S.ldmw, 32)
-    done(v.tensor_tensor(T.t1[:], T.msb[:], T.km[:], AluOpType.mult))
-    v.wait_ge(S.vec, nv[0])
-    done(v.tensor_tensor(T.bb[:], T.t1[:], T.wsb[:], AluOpType.add))
-    v.wait_ge(S.ldg, 16)
-    done(v.tensor_tensor(T.t2[:], T.gin[:, c0:c0 + F], T.kh[:, c0:c0 + F], AluOpType.mult))
-    if c0 > 0:
-        done(v.tensor_tensor(T.gsc[:, 0:c0], T.gin[:, 0:c0], T.kh[:, 0:c0], AluOpType.mult))
-    if c0 + F < N * F:
-        done(v.tensor_tensor(T.gsc[:, c0 + F:], T.gin[:, c0 + F:], T.kh[:, c0 + F:], AluOpType.mult))
-    v.wait_ge(S.vec, nv[0])
-    done(v.tensor_tensor(T.gsc[:, c0:c0 + F], T.t2[:], T.bb[:], AluOpType.add))
-
-    g.sync.wait_ge(S.vec, nv[0])
-    g.sync.dma_start(T.dsl[:], T.gsc[:]).then_inc(S.std, 16)
+    g.sync.wait_ge(S.ve, 1)
+    g.sync.wait_ge(S.cpl, 16)
+    g.sync.dma_start(T.dsl[late * HR + (c0 - late * HW) // PW:(late + 1) * HR:HW // PW, :], T.eb[:]).then_inc(S.stb, 16)
 
     sent = 0
-    g.wait_ge(S.std, 16)
-    tr = []
-    for k, d in enumerate(peers):
-        eng = _bits(topo.mask(core, d))[k]
-        tr.append(RemoteDMATransfer(dst_ids=[dst_id(d)], dma_engine_mask=eng, remote_sem=S.a1,
-                                    src=piece(T.dsl, q[d]), dst=piece(T.l1, slot(core, d))))
-        sent += 1
-    g.remote_dma_fused(tr, local_sem=S.snt)
+    for h, sem in ((early, S.cpe), (late, S.stb)):
+        g.wait_ge(sem, 16)
+        tr = []
+        for d in peers:
+            e = engines(core, d)
+            tr.append(RemoteDMATransfer(dst_ids=[dst_id(d)], dma_engine_mask=sum(e), remote_sem=S.a1,
+                                        src=piece(T.dsl, h, q[d]), dst=piece(T.l1, h, slot(core, d), PIECES - 1)))
+            sent += len(e)
+        g.remote_dma_fused(tr, local_sem=S.snt)
 
-    mine = [piece(T.l1, k) for k in range(PIECES - 1)] + [piece(T.dsl, me)]
-    g.wait_ge(S.a1, len(peers))
-    mfar = topo.mask(core, far)
-    g.remote_dma_fused([RemoteDMATransfer(dst_ids=[dst_id(far)], dma_engine_mask=mfar, remote_sem=S.a2,
-                                          srcs=mine, dsts=[T.cab[:]], alu_op=1)], local_sem=S.snt)
-    sent += _count(mfar)
-
-    g.wait_ge(S.a2, _count(topo.mask(far, core)))
+    mine = [[piece(T.l1, h, k, PIECES - 1) for k in range(PIECES - 1)] + [piece(T.dsl, h, me)] for h in range(H)]
+    g.wait_ge(S.a1, H * sum(len(engines(s, core)) for s in peers))
     outs = peers + [far]
-    mall = mfar
+    mall = topo.mask(core, far)
     for d in outs:
         mall &= topo.mask(core, d)
-    g.remote_dma_fused([RemoteDMATransfer(dst_ids=[dst_id(d) for d in outs], dma_engine_mask=mall, remote_sem=S.a3,
-                                          srcs=mine + [T.cab[:]], dsts=[piece(T.yall, me) for d in outs], alu_op=1)],
+    b = _bits(mall)
+    ne = len(b) // H
+    mh = [sum(b[h * ne:(h + 1) * ne]) for h in range(H)]
+    g.remote_dma_fused([RemoteDMATransfer(dst_ids=[dst_id(far)], dma_engine_mask=mh[h], remote_sem=S.a2,
+                                          srcs=mine[h], dsts=[piece(T.cab, h, 0, 1)], alu_op=1) for h in range(H)],
                        local_sem=S.snt)
-    sent += _count(mall)
+    sent += H * ne
 
-    got = len(outs) * _count(mall)
-    g.sync.wait_ge(S.a3, got)
-    g.sync.dma_start(T.y[:], T.yall[:]).then_inc(S.sty, 16)
-    per_row = N * F // PW
-    g.scalar.wait_ge(S.a3, got)
-    a0, b0 = c0 // PW, c0 % PW
-    g.scalar.dma_start(T.yb[:], T.yall[a0::per_row, b0:b0 + F]).then_inc(S.ldb, 16)
-    v.wait_ge(S.ldb, 16)
-    done(v.tensor_tensor(T.dd[:], T.wsb[:], T.yb[:], AluOpType.subtract))
-    v.wait_ge(S.vec, nv[0])
-    done(v.tensor_tensor(T.mob[:], T.dd[:], T.dd[:], AluOpType.add))
-    g.scalar.wait_ge(S.vec, nv[0])
-    g.scalar.dma_start(T.mo[:], T.mob[:]).then_inc(S.stm, 16)
+    g.wait_ge(S.a2, H * ne)
+    g.remote_dma_fused([RemoteDMATransfer(dst_ids=[dst_id(d) for d in outs], dma_engine_mask=mh[h], remote_sem=S.a3,
+                                          srcs=mine[h] + [piece(T.cab, h, 0, 1)],
+                                          dsts=[piece(T.tall, h, me) for d in outs], alu_op=1) for h in range(H)],
+                       local_sem=S.snt)
+    sent += H * ne
+
+    got = len(outs) * H * ne
+    qs = (g.sync, g.scalar)
+    lds = (S.ld0, S.ld1)
+    ps = (S.p0, S.p1)
+    for h in range(H):
+        qs[h].wait_ge(S.a3, got)
+        qs[h].dma_start(T.tt[:, h * HW:(h + 1) * HW], T.tall[h * HR:(h + 1) * HR, :]).then_inc(lds[h], 16)
+    for h in range(H):
+        v.wait_ge(lds[h], 16)
+        v.tensor_tensor(T.ysb[:, h * HW:(h + 1) * HW], T.tt[:, h * HW:(h + 1) * HW], T.kh[:, h * HW:(h + 1) * HW],
+                        AluOpType.mult).then_inc(ps[h], 1)
+        if h == late:
+            v.tensor_tensor(T.mob[:], T.tt[:, c0:c0 + F], T.xx[:, F:2 * F], AluOpType.subtract).then_inc(S.pm, 1)
+    for h in range(H):
+        qs[h].wait_ge(ps[h], 1)
+        qs[h].dma_start(T.y[:, h * HW:(h + 1) * HW], T.ysb[:, h * HW:(h + 1) * HW]).then_inc(S.sty, 16)
+    g.sync.wait_ge(S.pm, 1)
+    g.sync.dma_start(T.mo[:], T.mob[:]).then_inc(S.stm, 16)
 
     g.wait_ge(S.snt, sent)
-    g.wait_ge(S.sty, 16)
+    g.wait_ge(S.sty, 16 * H)
     g.wait_ge(S.stm, 16)

from concourse.bass import DstId, RemoteDMATransfer
from concourse.mybir import AluOpType

P = 128
N = 16
F = 32
H = 2
HW = N * F // H
PIECES = 8
PW = HW // PIECES
HR = PIECES * P

SCRATCH = {
    "mw": ("sbuf", [P, 2 * F], "bfloat16"),
    "gb": ("sbuf", [P, F], "bfloat16"),
    "kk": ("psum", [P, 2 * F], "float32"),
    "kh": ("psum", [P, N * F], "float32"),
    "xx": ("sbuf", [P, 2 * F], "float32"),
    "cc": ("sbuf", [P, F], "float32"),
    "eb": ("sbuf", [P, F], "bfloat16"),
    "tt": ("sbuf", [P, N * F], "bfloat16"),
    "ysb": ("sbuf", [P, N * F], "bfloat16"),
    "mob": ("sbuf", [P, F], "bfloat16"),
    "dsl": ("dram", [H * HR, PW], "bfloat16"),
    "l1": ("dram", [H * (PIECES - 1) * P, PW], "bfloat16"),
    "cab": ("dram", [H * P, PW], "bfloat16"),
    "tall": ("dram", [H * HR, PW], "bfloat16"),
}
SEMAPHORES = ["lmw", "lgb", "cpe", "cpl", "vec", "ve", "stb", "a1", "a2", "a3", "snt",
              "ld0", "ld1", "p0", "p1", "pm", "sty", "stm"]


def _bits(mask):
    return [1 << e for e in range(16) if (mask >> e) & 1]


def rank_program(g, core, T, topo):
    rank = T.rank_of(core)
    if rank is None:
        return
    cores = list(T.cores)
    S = T.sem

    def rack_of(c):
        return topo.rack(topo.host(c))

    def cable_peer(c):
        return [d for d in cores
                if rack_of(d) != rack_of(c) and topo.chip(d) == topo.chip(c) and topo.may_write(c, d)][0]

    def rack_peers(c):
        return [d for d in cores if d != c and topo.same_plane(c, d)]

    q = {}
    for c in cores:
        if rack_of(c) == rack_of(cores[0]):
            q[c] = len(q)
    for c in cores:
        if c not in q:
            q[c] = q[cable_peer(c)]
    peers = rack_peers(core)
    far = cable_peer(core)
    me = q[core]

    def piece(buf, h, k, n=PIECES):
        return buf[(h * n + k) * P:(h * n + k + 1) * P, :]

    def slot(sender, receiver):
        return q[sender] - (1 if q[sender] > q[receiver] else 0)

    def dst_id(d):
        rid, pid = topo.addr(d, core)
        return DstId(rid=rid, pnc=pid)

    def engines(s, d):
        ps = rack_peers(s)
        b = _bits(topo.mask(s, d))
        k = ps.index(d)
        return b[k:] if k == len(ps) - 1 else b[k:k + 1]

    c0 = rank * F
    late = c0 // HW
    early = 1 - late
    v = g.vector

    g.sync.dma_start(T.mw[:, 0:F], T.m[:]).then_inc(S.lmw, 16)
    g.scalar.dma_start(T.mw[:, F:2 * F], T.w[:]).then_inc(S.lmw, 16)
    g.scalar.dma_start(T.gb[:], T.gr[:, c0:c0 + F]).then_inc(S.lgb, 16)
    g.sync.dma_start(T.dsl[early * HR:(early + 1) * HR, :], T.gr[:, early * HW:(early + 1) * HW]).then_inc(S.cpe, 16)
    g.scalar.dma_start(T.dsl[late * HR:(late + 1) * HR, :], T.gr[:, late * HW:(late + 1) * HW]).then_inc(S.cpl, 16)

    v.memset(T.kk[:, 0:F], 0.75).then_inc(S.vec, 1)
    v.memset(T.kk[:, F:2 * F], -2.0).then_inc(S.vec, 1)
    v.memset(T.kh[:], -0.5).then_inc(S.vec, 1)
    v.wait_ge(S.vec, 3)
    v.wait_ge(S.lmw, 32)
    v.tensor_tensor(T.xx[:], T.mw[:], T.kk[:], AluOpType.mult).then_inc(S.vec, 1)
    v.wait_ge(S.vec, 4)
    v.tensor_tensor(T.cc[:], T.xx[:, 0:F], T.xx[:, F:2 * F], AluOpType.add).then_inc(S.vec, 1)
    v.wait_ge(S.vec, 5)
    v.wait_ge(S.lgb, 16)
    v.tensor_tensor(T.eb[:], T.gb[:], T.cc[:], AluOpType.add).then_inc(S.ve, 1)

    g.sync.wait_ge(S.ve, 1)
    g.sync.wait_ge(S.cpl, 16)
    g.sync.dma_start(T.dsl[late * HR + (c0 - late * HW) // PW:(late + 1) * HR:HW // PW, :], T.eb[:]).then_inc(S.stb, 16)

    sent = 0
    for h, sem in ((early, S.cpe), (late, S.stb)):
        g.wait_ge(sem, 16)
        tr = []
        for d in peers:
            e = engines(core, d)
            tr.append(RemoteDMATransfer(dst_ids=[dst_id(d)], dma_engine_mask=sum(e), remote_sem=S.a1,
                                        src=piece(T.dsl, h, q[d]), dst=piece(T.l1, h, slot(core, d), PIECES - 1)))
            sent += len(e)
        g.remote_dma_fused(tr, local_sem=S.snt)

    mine = [[piece(T.l1, h, k, PIECES - 1) for k in range(PIECES - 1)] + [piece(T.dsl, h, me)] for h in range(H)]
    g.wait_ge(S.a1, H * sum(len(engines(s, core)) for s in peers))
    outs = peers + [far]
    mall = topo.mask(core, far)
    for d in outs:
        mall &= topo.mask(core, d)
    b = _bits(mall)
    ne = len(b) // H
    mh = [sum(b[h * ne:(h + 1) * ne]) for h in range(H)]
    g.remote_dma_fused([RemoteDMATransfer(dst_ids=[dst_id(far)], dma_engine_mask=mh[h], remote_sem=S.a2,
                                          srcs=mine[h], dsts=[piece(T.cab, h, 0, 1)], alu_op=1) for h in range(H)],
                       local_sem=S.snt)
    sent += H * ne

    g.wait_ge(S.a2, H * ne)
    g.remote_dma_fused([RemoteDMATransfer(dst_ids=[dst_id(d) for d in outs], dma_engine_mask=mh[h], remote_sem=S.a3,
                                          srcs=mine[h] + [piece(T.cab, h, 0, 1)],
                                          dsts=[piece(T.tall, h, me) for d in outs], alu_op=1) for h in range(H)],
                       local_sem=S.snt)
    sent += H * ne

    got = len(outs) * H * ne
    qs = (g.sync, g.scalar)
    lds = (S.ld0, S.ld1)
    ps = (S.p0, S.p1)
    for h in range(H):
        qs[h].wait_ge(S.a3, got)
        qs[h].dma_start(T.tt[:, h * HW:(h + 1) * HW], T.tall[h * HR:(h + 1) * HR, :]).then_inc(lds[h], 16)
    for h in range(H):
        v.wait_ge(lds[h], 16)
        v.tensor_tensor(T.ysb[:, h * HW:(h + 1) * HW], T.tt[:, h * HW:(h + 1) * HW], T.kh[:, h * HW:(h + 1) * HW],
                        AluOpType.mult).then_inc(ps[h], 1)
        if h == late:
            v.tensor_tensor(T.mob[:], T.tt[:, c0:c0 + F], T.xx[:, F:2 * F], AluOpType.subtract).then_inc(S.pm, 1)
    for h in range(H):
        qs[h].wait_ge(ps[h], 1)
        qs[h].dma_start(T.y[:, h * HW:(h + 1) * HW], T.ysb[:, h * HW:(h + 1) * HW]).then_inc(S.sty, 16)
    g.sync.wait_ge(S.pm, 1)
    g.sync.dma_start(T.mo[:], T.mob[:]).then_inc(S.stm, 16)

    g.wait_ge(S.snt, sent)
    g.wait_ge(S.sty, 16 * H)
    g.wait_ge(S.stm, 16)
